import numpy as np, ml_dtypes
CORES = [21,109,149,237,277,365,405,493,150,406]
N = 10
DEG, TK = 3, 512
MASK = [[5,7,0],[5,7,1],[5,7,2],[5,7,3],[5,7,4],[5,7,0],[5,7,6],[5,7,0],[5,7,8],[5,7,9]]
def setup_inputs(rng):
    return {"x": rng.standard_normal((N, 128, TK), dtype=np.float32).astype(ml_dtypes.bfloat16), "w": rng.standard_normal((N, 128, DEG * 128), dtype=np.float32).astype(ml_dtypes.bfloat16)}
def setup_inputs_big(rng):
    d = setup_inputs(rng)
    for k in ("x", "w"): d[k] = (d[k].astype(np.float32) * 1024.0).astype(d[k].dtype)
    return d
def setup_inputs_small(rng):
    d = setup_inputs(rng)
    for k in ("x", "w"): d[k] = (d[k].astype(np.float32) * (1 / 1024.0)).astype(d[k].dtype)
    return d
def setup_inputs_apart(rng):
    d = setup_inputs(rng)
    f = (10.0 ** rng.permutation(np.linspace(-1.5, 1.5, N))).astype(np.float32).reshape(N, 1, 1)
    for k in ("x", "w"): d[k] = (d[k].astype(np.float32) * f).astype(d[k].dtype)
    return d
def reference(x, w):
    X, W = x.astype(np.float64), w.astype(np.float64)
    y = np.zeros((N, 128, TK))
    for r in range(N):
        for i, j in enumerate(MASK[r]):
            y[r] += W[r][:, 128 * i:128 * i + 128].T @ X[j]
    return {"y": y.astype(ml_dtypes.bfloat16 if x.dtype != np.float64 else np.float64)}

@@ -1,0 +1,185 @@
+from concourse.bass import DstId, RemoteDMATransfer
+
+SIM_CORES = 512
+P, COLS, TILE = 128, 512, 128
+
+SCRATCH = {
+    "stage": ("dram", [P, COLS], "bfloat16"),
+    "xs": ("sbuf", [P, COLS], "bfloat16"),
+    "ws": ("sbuf", [P, 3 * TILE], "bfloat16"),
+    "in0": ("sbuf", [P, COLS], "bfloat16"),
+    "in1": ("sbuf", [P, COLS], "bfloat16"),
+    "ys": ("sbuf", [P, COLS], "bfloat16"),
+    "acc": ("psum", [P, COLS], "float32"),
+}
+SEMAPHORES = ["ld_s", "ld_x", "ld_w", "a0", "a1", "a2", "sent", "mm", "cp", "st"]
+
+_CACHE = {}
+
+
+def _bits(m):
+    return [b for b in range(m.bit_length()) if (m >> b) & 1]
+
+
+def _plan(T, topo):
+    cores = list(T.cores)
+    group = set(cores)
+    table = T.tables["MASK"]
+    n = len(cores)
+    world = range(SIM_CORES)
+
+    def place(c):
+        return (topo.host(c), topo.chip(c))
+
+    def rack(c):
+        return topo.rack(topo.host(c))
+
+    sources = [j for j in range(n) if any(j in table[r] for r in range(n) if r != j)]
+    used = set()
+    steps = {}
+    depth = {}
+
+    def relay(at, die, feeder, targets):
+        cand = [c for c in world if place(c) == place(at) and c not in group and c not in used
+                and topo.may_write(feeder, c) and all(topo.may_write(c, t) for t in targets)]
+        cand.sort(key=lambda c: (topo.die(c) != die, c))
+        used.add(cand[0])
+        return cand[0]
+
+    def add(core, j, calls):
+        steps.setdefault(core, []).append((j, calls))
+        for call in calls:
+            for d in call:
+                depth[(d, j)] = depth[(core, j)] + 1
+
+    for k, j in enumerate(sources):
+        s = cores[j]
+        depth[(s, j)] = 0
+        cons = sorted(cores[r] for r in range(n) if r != j and j in table[r])
+        own = topo.die(s)
+        other = [d for d in sorted({topo.die(c) for c in world if place(c) == place(s)}) if d != own][0]
+        d_first, d_second = (other, own) if k % 2 else (own, other)
+
+        near = [d for d in cons if rack(d) == rack(s)]
+        far = [d for d in cons if rack(d) != rack(s)]
+        direct = [d for d in near if topo.may_write(s, d)]
+        cross = [d for d in near if not topo.may_write(s, d)]
+        later = []
+        jobs = {"G": [], "Ha": cross[0::2], "J": [], "Hb": cross[1::2]}
+        home = {"Ha": s, "Hb": s}
+        forward = []
+        far_direct = []
+        if far:
+            entry = [c for c in world if rack(c) != rack(s) and topo.chip(c) == topo.chip(s) and topo.may_write(s, c)]
+            home["G"] = entry[0]
+            far_direct = [d for d in far if place(d) == place(entry[0])]
+            rest = [d for d in far if d not in far_direct]
+            if direct:
+                forward = [d for d in rest if topo.may_write(direct[0], d)]
+                rest = [d for d in rest if d not in forward]
+                beyond = [d for d in rest if topo.host(d) != topo.host(entry[0])]
+                if len(rest) > 2 and beyond:
+                    jobs["J"] = beyond[:1]
+                    home["J"] = direct[0]
+                    rest = [d for d in rest if d not in jobs["J"]]
+            jobs["G"] = rest
+        dies = {"G": d_first, "Ha": d_first, "J": d_first, "Hb": d_second}
+        for name in ("G", "Ha", "J", "Hb"):
+            if jobs[name]:
+                later.append((relay(home[name], dies[name], s, jobs[name]), jobs[name]))
+        feeds = [h for h, _ in later]
+        calls = [feeds[i:i + 2] for i in range(0, len(feeds), 2)] + [[d] for d in direct + far_direct]
+        add(s, j, calls)
+        for h, targets in later:
+            add(h, j, [targets])
+        if forward:
+            add(direct[0], j, [[d] for d in forward])
+
+    engines = {}
+    arrive = {}
+    for c, todo in steps.items():
+        todo.sort(key=lambda e: depth[(c, e[0])])
+        m = -1
+        for _, calls in todo:
+            for call in calls:
+                for d in call:
+                    m &= topo.mask(c, d)
+        engines[c] = _bits(m)
+        for j, calls in todo:
+            for call in calls:
+                for d in call:
+                    arrive[(d, j)] = len(engines[c]) // len(call)
+    return {"steps": steps, "engines": engines, "arrive": arrive, "depth": depth,
+            "sem": {j: "a%d" % k for k, j in enumerate(sources)}}
+
+
+def rank_program(g, core, T, topo):
+    if "plan" not in _CACHE:
+        _CACHE["plan"] = _plan(T, topo)
+    plan = _CACHE["plan"]
+    table = T.tables["MASK"]
+    rank = T.rank_of(core)
+    todo = plan["steps"].get(core, [])
+    if rank is None and not todo:
+        return
+    sem = T.sem
+
+    def landing(c, j):
+        r = T.rank_of(c)
+        if r is None:
+            return T.stage[:]
+        return T["in%d" % [m for m in table[r] if m != r].index(j)][:]
+
+    if rank is not None:
+        if any(j == rank for j, _ in todo):
+            g.sync.dma_start(T.stage[:], T.x[:]).then_inc(sem.ld_s, 16)
+            g.scalar.dma_start(T.xs[:], T.x[:]).then_inc(sem.ld_x, 16)
+            g.sync.dma_start(T.ws[:], T.w[:]).then_inc(sem.ld_w, 16)
+        else:
+            g.sync.dma_start(T.xs[:], T.x[:]).then_inc(sem.ld_x, 16)
+            g.scalar.dma_start(T.ws[:], T.w[:]).then_inc(sem.ld_w, 16)
+
+    eng = plan["engines"].get(core, [])
+    sent = 0
+    for j, calls in todo:
+        if j == rank:
+            g.wait_ge(sem.ld_s, 16)
+            src = T.stage[:]
+        else:
+            g.wait_ge(sem[plan["sem"][j]], plan["arrive"][(core, j)])
+            src = landing(core, j)
+        for call in calls:
+            share = len(eng) // len(call)
+            transfers = []
+            for i, d in enumerate(call):
+                rid, pid = topo.addr(d, core)
+                transfers.append(RemoteDMATransfer(
+                    dst_ids=[DstId(rid=rid, pnc=pid)],
+                    dma_engine_mask=sum(1 << b for b in eng[i * share:(i + 1) * share]),
+                    remote_sem=sem[plan["sem"][j]], src=src, dst=landing(d, j)))
+                sent += share
+            g.remote_dma_fused(transfers, local_sem=sem.sent)
+    if sent:
+        g.wait_ge(sem.sent, sent)
+
+    if rank is None:
+        return
+    order = sorted(range(len(table[rank])), key=lambda i: plan["depth"].get((core, table[rank][i]), 0)
+                   if table[rank][i] != rank else -1)
+    g.tensor.wait_ge(sem.ld_w, 16)
+    for pos, i in enumerate(order):
+        j = table[rank][i]
+        if j == rank:
+            g.tensor.wait_ge(sem.ld_x, 16)
+            rhs = T.xs[:]
+        else:
+            g.tensor.wait_ge(sem[plan["sem"][j]], plan["arrive"][(core, j)])
+            rhs = landing(core, j)
+        mm = g.tensor.matmul(T.acc[:], T.ws[:, TILE * i:TILE * (i + 1)], rhs,
+                             start=(pos == 0), stop=(pos == len(order) - 1))
+    mm.then_inc(sem.mm, 1)
+    g.vector.wait_ge(sem.mm, 1)
+    g.vector.tensor_copy(T.ys[:], T.acc[:]).then_inc(sem.cp, 1)
+    g.sync.wait_ge(sem.cp, 1)
+    g.sync.dma_start(T.y[:], T.ys[:]).then_inc(sem.st, 16)
+    g.sync.wait_ge(sem.st, 16)

@@ -49,8 +49,9 @@ def _plan(T, topo):
     def add(core, j, calls):
         steps.setdefault(core, []).append((j, calls))
         for call in calls:
-            for d in call:
-                depth[(d, j)] = depth[(core, j)] + 1
+            for transfer in call:
+                for d in transfer:
+                    depth[(d, j)] = depth[(core, j)] + 1
 
     for k, j in enumerate(sources):
         s = cores[j]
@@ -64,36 +65,30 @@ def _plan(T, topo):
         far = [d for d in cons if rack(d) != rack(s)]
         direct = [d for d in near if topo.may_write(s, d)]
         cross = [d for d in near if not topo.may_write(s, d)]
-        later = []
         jobs = {"G": [], "Ha": cross[0::2], "J": [], "Hb": cross[1::2]}
         home = {"Ha": s, "Hb": s}
-        forward = []
-        far_direct = []
         if far:
             entry = [c for c in world if rack(c) != rack(s) and topo.chip(c) == topo.chip(s) and topo.may_write(s, c)]
             home["G"] = entry[0]
-            far_direct = [d for d in far if place(d) == place(entry[0])]
-            rest = [d for d in far if d not in far_direct]
-            if direct:
-                forward = [d for d in rest if topo.may_write(direct[0], d)]
-                rest = [d for d in rest if d not in forward]
-                beyond = [d for d in rest if topo.host(d) != topo.host(entry[0])]
-                if len(rest) > 2 and beyond:
-                    jobs["J"] = beyond[:1]
-                    home["J"] = direct[0]
-                    rest = [d for d in rest if d not in jobs["J"]]
-            jobs["G"] = rest
+            at_entry = [d for d in far if place(d) == place(entry[0])]
+            rest = [d for d in far if d not in at_entry]
+            plain = [d for d in rest if topo.same_plane(entry[0], d)]
+            rest = [d for d in rest if d not in plain]
+            beyond = [d for d in rest if topo.host(d) != topo.host(entry[0])]
+            if direct and len(rest) > 2 and beyond:
+                jobs["J"] = beyond[:1]
+                home["J"] = direct[0]
+                rest = [d for d in rest if d not in jobs["J"]]
+            jobs["G"] = rest + plain + at_entry
         dies = {"G": d_first, "Ha": d_first, "J": d_first, "Hb": d_second}
+        later = []
         for name in ("G", "Ha", "J", "Hb"):
             if jobs[name]:
                 later.append((relay(home[name], dies[name], s, jobs[name]), jobs[name]))
-        feeds = [h for h, _ in later]
-        calls = [feeds[i:i + 2] for i in range(0, len(feeds), 2)] + [[d] for d in direct + far_direct]
-        add(s, j, calls)
+        feeds = [[h] for h, _ in later]
+        add(s, j, [feeds[i:i + 2] for i in range(0, len(feeds), 2)] + [[[d]] for d in direct])
         for h, targets in later:
-            add(h, j, [targets])
-        if forward:
-            add(direct[0], j, [[d] for d in forward])
+            add(h, j, [[t for t in (targets[0::2], targets[1::2]) if t]])
 
     engines = {}
     arrive = {}
@@ -102,13 +97,15 @@ def _plan(T, topo):
         m = -1
         for _, calls in todo:
             for call in calls:
-                for d in call:
-                    m &= topo.mask(c, d)
+                for transfer in call:
+                    for d in transfer:
+                        m &= topo.mask(c, d)
         engines[c] = _bits(m)
         for j, calls in todo:
             for call in calls:
-                for d in call:
-                    arrive[(d, j)] = len(engines[c]) // len(call)
+                for transfer in call:
+                    for d in transfer:
+                        arrive[(d, j)] = len(engines[c]) // len(call)
     return {"steps": steps, "engines": engines, "arrive": arrive, "depth": depth,
             "sem": {j: "a%d" % k for k, j in enumerate(sources)}}
 
@@ -151,12 +148,12 @@ def rank_program(g, core, T, topo):
         for call in calls:
             share = len(eng) // len(call)
             transfers = []
-            for i, d in enumerate(call):
-                rid, pid = topo.addr(d, core)
+            for i, dests in enumerate(call):
+                ids = [topo.addr(d, core) for d in dests]
                 transfers.append(RemoteDMATransfer(
-                    dst_ids=[DstId(rid=rid, pnc=pid)],
+                    dst_ids=[DstId(rid=rid, pnc=pid) for rid, pid in ids],
                     dma_engine_mask=sum(1 << b for b in eng[i * share:(i + 1) * share]),
-                    remote_sem=sem[plan["sem"][j]], src=src, dst=landing(d, j)))
+                    remote_sem=sem[plan["sem"][j]], srcs=[src], dsts=[landing(d, j) for d in dests]))
                 sent += share
             g.remote_dma_fused(transfers, local_sem=sem.sent)
     if sent:

@@ -2,6 +2,10 @@ from concourse.bass import DstId, RemoteDMATransfer
 
 SIM_CORES = 512
 P, COLS, TILE = 128, 512, 128
+NFAR = 2
+PARTS = [64, 64, 192, 192]
+STARTS = [sum(PARTS[:i]) for i in range(len(PARTS))]
+NSRC = 3
 
 SCRATCH = {
     "stage": ("dram", [P, COLS], "bfloat16"),
@@ -12,7 +16,11 @@ SCRATCH = {
     "ys": ("sbuf", [P, COLS], "bfloat16"),
     "acc": ("psum", [P, COLS], "float32"),
 }
-SEMAPHORES = ["ld_s", "ld_x", "ld_w", "a0", "a1", "a2", "sent", "mm", "cp", "st"]
+for _i, _w in enumerate(PARTS):
+    SCRATCH["part%d" % _i] = ("dram", [P, _w], "bfloat16")
+SEMAPHORES = (["ld_s", "ld_x", "ld_w", "sent", "mm", "cp", "st"] + ["a%d" % k for k in range(NSRC)]
+              + ["l%d" % p for p in range(len(PARTS))]
+              + ["f%d_%d" % (k, p) for k in range(NSRC) for p in range(len(PARTS))])
 
 _CACHE = {}
 
@@ -34,6 +42,12 @@ def _plan(T, topo):
     def rack(c):
         return topo.rack(topo.host(c))
 
+    def common(c, dests):
+        m = -1
+        for d in dests:
+            m &= topo.mask(c, d)
+        return _bits(m)
+
     sources = [j for j in range(n) if any(j in table[r] for r in range(n) if r != j)]
     used = set()
     steps = {}
@@ -46,16 +60,22 @@ def _plan(T, topo):
         used.add(cand[0])
         return cand[0]
 
-    def add(core, j, calls):
-        steps.setdefault(core, []).append((j, calls))
-        for call in calls:
-            for transfer in call:
-                for d in transfer:
-                    depth[(d, j)] = depth[(core, j)] + 1
+    def fan(h, targets, part, name):
+        away = [t for t in targets if place(t) != place(h)]
+        here = [t for t in targets if place(t) == place(h)]
+        eng = common(h, away)
+        half = len(eng) // 2
+        lists = [t for t in (away[0::2], away[1::2]) if t]
+        call = [(eng if len(lists) == 1 else eng[i * half:(i + 1) * half], t, part, name)
+                for i, t in enumerate(lists)]
+        if here:
+            spare = [b for b in common(h, here) if b not in eng]
+            call.append((spare[:len(eng) // 4], here, part, name))
+        return call
 
     for k, j in enumerate(sources):
         s = cores[j]
-        depth[(s, j)] = 0
+        name = "a%d" % k
         cons = sorted(cores[r] for r in range(n) if r != j and j in table[r])
         own = topo.die(s)
         other = [d for d in sorted({topo.die(c) for c in world if place(c) == place(s)}) if d != own][0]
@@ -65,49 +85,42 @@ def _plan(T, topo):
         far = [d for d in cons if rack(d) != rack(s)]
         direct = [d for d in near if topo.may_write(s, d)]
         cross = [d for d in near if not topo.may_write(s, d)]
-        jobs = {"G": [], "Ha": cross[0::2], "J": [], "Hb": cross[1::2]}
-        home = {"Ha": s, "Hb": s}
+        for d in cons:
+            depth[(d, j)] = 1 if d in direct else 2
+        entry = [c for c in world if rack(c) != rack(s) and topo.chip(c) == topo.chip(s) and topo.may_write(s, c)]
+        eng = common(s, entry[:1])
+        cable, local = eng[:len(eng) // 2], eng[len(eng) // 2:]
+        heads, bodies, feeds = [], [], []
         if far:
-            entry = [c for c in world if rack(c) != rack(s) and topo.chip(c) == topo.chip(s) and topo.may_write(s, c)]
-            home["G"] = entry[0]
-            at_entry = [d for d in far if place(d) == place(entry[0])]
-            rest = [d for d in far if d not in at_entry]
-            plain = [d for d in rest if topo.same_plane(entry[0], d)]
-            rest = [d for d in rest if d not in plain]
-            beyond = [d for d in rest if topo.host(d) != topo.host(entry[0])]
-            if direct and len(rest) > 2 and beyond:
-                jobs["J"] = beyond[:1]
-                home["J"] = direct[0]
-                rest = [d for d in rest if d not in jobs["J"]]
-            jobs["G"] = rest + plain + at_entry
-        dies = {"G": d_first, "Ha": d_first, "J": d_first, "Hb": d_second}
-        later = []
-        for name in ("G", "Ha", "J", "Hb"):
-            if jobs[name]:
-                later.append((relay(home[name], dies[name], s, jobs[name]), jobs[name]))
-        feeds = [[h] for h, _ in later]
-        add(s, j, [feeds[i:i + 2] for i in range(0, len(feeds), 2)] + [[[d]] for d in direct])
-        for h, targets in later:
-            add(h, j, [[t for t in (targets[0::2], targets[1::2]) if t]])
+            G = [relay(entry[0], die, s, far) for die in (d_first, d_second)][:NFAR]
+            share = len(cable) // NFAR
+            for p in range(len(PARTS)):
+                f = "f%d_%d" % (k, p)
+                if p < NFAR:
+                    heads.append((cable[p * share:(p + 1) * share], [G[p]], p, f))
+                    got = share
+                else:
+                    bodies.append([(cable, [G[p % NFAR]], p, f)])
+                    got = len(cable)
+                steps.setdefault(G[p % NFAR], []).append(((f, got), fan(G[p % NFAR], far, p, name)))
+        for targets, die in ((cross[0::2], d_first), (cross[1::2], d_second)):
+            if targets:
+                H = relay(s, die, s, targets)
+                mine = local if not feeds else [b for b in common(s, [H]) if b not in eng][:len(local)]
+                feeds.append((mine, [H], None, name))
+                steps.setdefault(H, []).append(((name, len(mine)), fan(H, targets, None, name)))
+        calls = [c for c in [heads, feeds] if c] + bodies + [[(local, [d], None, name)] for d in direct]
+        steps.setdefault(s, []).extend((None, call) for call in calls)
 
-    engines = {}
     arrive = {}
     for c, todo in steps.items():
-        todo.sort(key=lambda e: depth[(c, e[0])])
-        m = -1
-        for _, calls in todo:
-            for call in calls:
-                for transfer in call:
-                    for d in transfer:
-                        m &= topo.mask(c, d)
-        engines[c] = _bits(m)
-        for j, calls in todo:
-            for call in calls:
-                for transfer in call:
-                    for d in transfer:
-                        arrive[(d, j)] = len(engines[c]) // len(call)
-    return {"steps": steps, "engines": engines, "arrive": arrive, "depth": depth,
-            "sem": {j: "a%d" % k for k, j in enumerate(sources)}}
+        for _, call in todo:
+            for eng, dests, _, name in call:
+                for d in dests:
+                    if d in group:
+                        arrive[(d, name)] = arrive.get((d, name), 0) + len(eng)
+    return {"steps": steps, "arrive": arrive, "depth": depth, "sem": {j: "a%d" % k for k, j in enumerate(sources)},
+            "src": {"a%d" % k: j for k, j in enumerate(sources)}}
 
 
 def rank_program(g, core, T, topo):
@@ -123,46 +136,60 @@ def rank_program(g, core, T, topo):
 
     def landing(c, j):
         r = T.rank_of(c)
-        if r is None:
-            return T.stage[:]
-        return T["in%d" % [m for m in table[r] if m != r].index(j)][:]
+        return T["in%d" % [m for m in table[r] if m != r].index(j)]
+
+    def whole_or_part(part):
+        return T.stage[:] if part is None else T["part%d" % part][:]
+
+    def staged(part):
+        return sem.ld_s if part is None else sem["l%d" % part]
 
     if rank is not None:
-        if any(j == rank for j, _ in todo):
-            g.sync.dma_start(T.stage[:], T.x[:]).then_inc(sem.ld_s, 16)
-            g.scalar.dma_start(T.xs[:], T.x[:]).then_inc(sem.ld_x, 16)
-            g.sync.dma_start(T.ws[:], T.w[:]).then_inc(sem.ld_w, 16)
-        else:
-            g.sync.dma_start(T.xs[:], T.x[:]).then_inc(sem.ld_x, 16)
-            g.scalar.dma_start(T.ws[:], T.w[:]).then_inc(sem.ld_w, 16)
+        pieces = []
+        for _, call in todo:
+            for t in call:
+                if t[2] not in pieces:
+                    pieces.append(t[2])
+        queues = [g.sync, g.scalar]
+        for q, p in enumerate(pieces):
+            cols = T.x[:] if p is None else T.x[:, STARTS[p]:STARTS[p] + PARTS[p]]
+            queues[q % 2].dma_start(whole_or_part(p), cols).then_inc(staged(p), 16)
+        queues[len(pieces) % 2].dma_start(T.xs[:], T.x[:]).then_inc(sem.ld_x, 16)
+        queues[(len(pieces) + 1) % 2].dma_start(T.ws[:], T.w[:]).then_inc(sem.ld_w, 16)
 
-    eng = plan["engines"].get(core, [])
     sent = 0
-    for j, calls in todo:
-        if j == rank:
-            g.wait_ge(sem.ld_s, 16)
-            src = T.stage[:]
+    waited = []
+    for wait, call in todo:
+        if wait is None:
+            for t in call:
+                if t[2] not in waited:
+                    waited.append(t[2])
+                    g.wait_ge(staged(t[2]), 16)
         else:
-            g.wait_ge(sem[plan["sem"][j]], plan["arrive"][(core, j)])
-            src = landing(core, j)
-        for call in calls:
-            share = len(eng) // len(call)
-            transfers = []
-            for i, dests in enumerate(call):
-                ids = [topo.addr(d, core) for d in dests]
-                transfers.append(RemoteDMATransfer(
-                    dst_ids=[DstId(rid=rid, pnc=pid) for rid, pid in ids],
-                    dma_engine_mask=sum(1 << b for b in eng[i * share:(i + 1) * share]),
-                    remote_sem=sem[plan["sem"][j]], srcs=[src], dsts=[landing(d, j) for d in dests]))
-                sent += share
-            g.remote_dma_fused(transfers, local_sem=sem.sent)
+            g.wait_ge(sem[wait[0]], wait[1])
+        transfers = []
+        for eng, dests, part, name in call:
+            dsts = []
+            for d in dests:
+                if T.rank_of(d) is None:
+                    dsts.append(whole_or_part(part))
+                elif part is None:
+                    dsts.append(landing(d, plan["src"][name])[:])
+                else:
+                    dsts.append(landing(d, plan["src"][name])[:, STARTS[part]:STARTS[part] + PARTS[part]])
+            ids = [topo.addr(d, core) for d in dests]
+            transfers.append(RemoteDMATransfer(
+                dst_ids=[DstId(rid=rid, pnc=pid) for rid, pid in ids],
+                dma_engine_mask=sum(1 << b for b in eng),
+                remote_sem=sem[name], srcs=[whole_or_part(part)], dsts=dsts))
+            sent += len(eng)
+        g.remote_dma_fused(transfers, local_sem=sem.sent)
     if sent:
         g.wait_ge(sem.sent, sent)
 
     if rank is None:
         return
-    order = sorted(range(len(table[rank])), key=lambda i: plan["depth"].get((core, table[rank][i]), 0)
-                   if table[rank][i] != rank else -1)
+    order = sorted(range(len(table[rank])), key=lambda i: plan["depth"].get((core, table[rank][i]), 0))
     g.tensor.wait_ge(sem.ld_w, 16)
     for pos, i in enumerate(order):
         j = table[rank][i]
@@ -170,8 +197,8 @@ def rank_program(g, core, T, topo):
             g.tensor.wait_ge(sem.ld_x, 16)
             rhs = T.xs[:]
         else:
-            g.tensor.wait_ge(sem[plan["sem"][j]], plan["arrive"][(core, j)])
-            rhs = landing(core, j)
+            g.tensor.wait_ge(sem[plan["sem"][j]], plan["arrive"][(core, plan["sem"][j])])
+            rhs = landing(core, j)[:]
         mm = g.tensor.matmul(T.acc[:], T.ws[:, TILE * i:TILE * (i + 1)], rhs,
                              start=(pos == 0), stop=(pos == len(order) - 1))
     mm.then_inc(sem.mm, 1)

@@ -2,8 +2,10 @@ from concourse.bass import DstId, RemoteDMATransfer
 
 SIM_CORES = 512
 P, COLS, TILE = 128, 512, 128
-NFAR = 2
-PARTS = [64, 64, 192, 192]
+HALF = COLS // 2
+NREL = 4
+NHEAD = 4
+PARTS = [32, 32, 32, 32, 112, 104, 96, 72]
 STARTS = [sum(PARTS[:i]) for i in range(len(PARTS))]
 NSRC = 3
 
@@ -14,12 +16,13 @@ SCRATCH = {
     "in0": ("sbuf", [P, COLS], "bfloat16"),
     "in1": ("sbuf", [P, COLS], "bfloat16"),
     "ys": ("sbuf", [P, COLS], "bfloat16"),
-    "acc": ("psum", [P, COLS], "float32"),
+    "acc0": ("psum", [P, COLS], "float32"),
+    "acc1": ("psum", [P, COLS], "float32"),
 }
 for _i, _w in enumerate(PARTS):
     SCRATCH["part%d" % _i] = ("dram", [P, _w], "bfloat16")
-SEMAPHORES = (["ld_s", "ld_x", "ld_w", "sent", "mm", "cp", "st"] + ["a%d" % k for k in range(NSRC)]
-              + ["l%d" % p for p in range(len(PARTS))]
+SEMAPHORES = (["ld_s", "ld_x", "ld_w", "sent", "mm0", "mm1", "cp0", "cp1", "st0", "st1"]
+              + ["a%d" % k for k in range(NSRC)] + ["l%d" % p for p in range(len(PARTS))]
               + ["f%d_%d" % (k, p) for k in range(NSRC) for p in range(len(PARTS))])
 
 _CACHE = {}
@@ -53,21 +56,26 @@ def _plan(T, topo):
     steps = {}
     depth = {}
 
-    def relay(at, die, feeder, targets):
-        cand = [c for c in world if place(c) == place(at) and c not in group and c not in used
-                and topo.may_write(feeder, c) and all(topo.may_write(c, t) for t in targets)]
-        cand.sort(key=lambda c: (topo.die(c) != die, c))
-        used.add(cand[0])
-        return cand[0]
+    def team(at, dies, feeder, targets):
+        out = []
+        for i in range(NREL):
+            cand = [c for c in world if place(c) == place(at) and c not in group and c not in used
+                    and topo.may_write(feeder, c) and all(topo.may_write(c, t) for t in targets)]
+            if cand:
+                cand.sort(key=lambda c: (topo.die(c) != dies[i % len(dies)], c))
+                used.add(cand[0])
+                out.append(cand[0])
+        return out
 
     def fan(h, targets, part, name):
         away = [t for t in targets if place(t) != place(h)]
         here = [t for t in targets if place(t) == place(h)]
         eng = common(h, away)
         half = len(eng) // 2
-        lists = [t for t in (away[0::2], away[1::2]) if t]
-        call = [(eng if len(lists) == 1 else eng[i * half:(i + 1) * half], t, part, name)
-                for i, t in enumerate(lists)]
+        if len(away) % 2:
+            call = [(eng, away, part, name)]
+        else:
+            call = [(eng[:half], away[0::2], part, name), (eng[half:], away[1::2], part, name)]
         if here:
             spare = [b for b in common(h, here) if b not in eng]
             call.append((spare[:len(eng) // 4], here, part, name))
@@ -79,7 +87,7 @@ def _plan(T, topo):
         cons = sorted(cores[r] for r in range(n) if r != j and j in table[r])
         own = topo.die(s)
         other = [d for d in sorted({topo.die(c) for c in world if place(c) == place(s)}) if d != own][0]
-        d_first, d_second = (other, own) if k % 2 else (own, other)
+        dies = (other, own) if k % 2 else (own, other)
 
         near = [d for d in cons if rack(d) == rack(s)]
         far = [d for d in cons if rack(d) != rack(s)]
@@ -90,26 +98,23 @@ def _plan(T, topo):
         entry = [c for c in world if rack(c) != rack(s) and topo.chip(c) == topo.chip(s) and topo.may_write(s, c)]
         eng = common(s, entry[:1])
         cable, local = eng[:len(eng) // 2], eng[len(eng) // 2:]
-        heads, bodies, feeds = [], [], []
+        teams = []
         if far:
-            G = [relay(entry[0], die, s, far) for die in (d_first, d_second)][:NFAR]
-            share = len(cable) // NFAR
-            for p in range(len(PARTS)):
-                f = "f%d_%d" % (k, p)
-                if p < NFAR:
-                    heads.append((cable[p * share:(p + 1) * share], [G[p]], p, f))
-                    got = share
-                else:
-                    bodies.append([(cable, [G[p % NFAR]], p, f)])
-                    got = len(cable)
-                steps.setdefault(G[p % NFAR], []).append(((f, got), fan(G[p % NFAR], far, p, name)))
-        for targets, die in ((cross[0::2], d_first), (cross[1::2], d_second)):
-            if targets:
-                H = relay(s, die, s, targets)
-                mine = local if not feeds else [b for b in common(s, [H]) if b not in eng][:len(local)]
-                feeds.append((mine, [H], None, name))
-                steps.setdefault(H, []).append(((name, len(mine)), fan(H, targets, None, name)))
-        calls = [c for c in [heads, feeds] if c] + bodies + [[(local, [d], None, name)] for d in direct]
+            teams.append((team(entry[0], dies, s, far), cable, far))
+        if cross:
+            teams.append((team(s, dies, s, cross), local, cross))
+        heads, bodies = [], []
+        for p in range(len(PARTS)):
+            f = "f%d_%d" % (k, p)
+            if p >= NHEAD:
+                bodies.append([])
+            for relays, mine, targets in teams:
+                h = relays[p % len(relays)]
+                share = len(mine) // NHEAD
+                use = mine[p * share:(p + 1) * share] if p < NHEAD else mine
+                (heads if p < NHEAD else bodies[-1]).append((use, [h], p, f))
+                steps.setdefault(h, []).append(((f, len(use)), fan(h, targets, p, name)))
+        calls = [heads] + bodies + [[(local, [d], None, name)] for d in direct]
         steps.setdefault(s, []).extend((None, call) for call in calls)
 
     arrive = {}
@@ -144,13 +149,13 @@ def rank_program(g, core, T, topo):
     def staged(part):
         return sem.ld_s if part is None else sem["l%d" % part]
 
+    queues = [g.sync, g.scalar]
     if rank is not None:
         pieces = []
         for _, call in todo:
             for t in call:
                 if t[2] not in pieces:
                     pieces.append(t[2])
-        queues = [g.sync, g.scalar]
         for q, p in enumerate(pieces):
             cols = T.x[:] if p is None else T.x[:, STARTS[p]:STARTS[p] + PARTS[p]]
             queues[q % 2].dma_start(whole_or_part(p), cols).then_inc(staged(p), 16)
@@ -195,15 +200,20 @@ def rank_program(g, core, T, topo):
         j = table[rank][i]
         if j == rank:
             g.tensor.wait_ge(sem.ld_x, 16)
-            rhs = T.xs[:]
+            rhs = T.xs
         else:
             g.tensor.wait_ge(sem[plan["sem"][j]], plan["arrive"][(core, plan["sem"][j])])
-            rhs = landing(core, j)[:]
-        mm = g.tensor.matmul(T.acc[:], T.ws[:, TILE * i:TILE * (i + 1)], rhs,
-                             start=(pos == 0), stop=(pos == len(order) - 1))
-    mm.then_inc(sem.mm, 1)
-    g.vector.wait_ge(sem.mm, 1)
-    g.vector.tensor_copy(T.ys[:], T.acc[:]).then_inc(sem.cp, 1)
-    g.sync.wait_ge(sem.cp, 1)
-    g.sync.dma_start(T.y[:], T.ys[:]).then_inc(sem.st, 16)
-    g.sync.wait_ge(sem.st, 16)
+            rhs = landing(core, j)
+        for h in range(2):
+            mm = g.tensor.matmul(T["acc%d" % h][:, 0:HALF], T.ws[:, TILE * i:TILE * (i + 1)],
+                                 rhs[:, HALF * h:HALF * (h + 1)], start=(pos == 0), stop=(pos == len(order) - 1))
+            if pos == len(order) - 1:
+                mm.then_inc(sem["mm%d" % h], 1)
+    for h in range(2):
+        g.vector.wait_ge(sem["mm%d" % h], 1)
+        g.vector.tensor_copy(T.ys[:, HALF * h:HALF * (h + 1)], T["acc%d" % h][:, 0:HALF]).then_inc(sem["cp%d" % h], 1)
+    for h in range(2):
+        queues[h].wait_ge(sem["cp%d" % h], 1)
+        queues[h].dma_start(T.y[:, HALF * h:HALF * (h + 1)],
+                            T.ys[:, HALF * h:HALF * (h + 1)]).then_inc(sem["st%d" % h], 16)
+        queues[h].wait_ge(sem["st%d" % h], 16)

@@ -2,11 +2,16 @@ from concourse.bass import DstId, RemoteDMATransfer
 
 SIM_CORES = 512
 P, COLS, TILE = 128, 512, 128
-HALF = COLS // 2
 NREL = 4
 NHEAD = 4
-PARTS = [32, 32, 32, 32, 112, 104, 96, 72]
+PARTS = [32, 32, 32, 32, 80, 64, 120, 120]
+DELEG = (6, 7)
 STARTS = [sum(PARTS[:i]) for i in range(len(PARTS))]
+GROUPS = [list(range(NHEAD))] + [[p] for p in range(NHEAD, len(PARTS))]
+GROUP_OF = {p: i for i, ps in enumerate(GROUPS) for p in ps}
+GSTART = [STARTS[ps[0]] for ps in GROUPS]
+GWIDTH = [sum(PARTS[p] for p in ps) for ps in GROUPS]
+NG = len(GROUPS)
 NSRC = 3
 
 SCRATCH = {
@@ -16,13 +21,15 @@ SCRATCH = {
     "in0": ("sbuf", [P, COLS], "bfloat16"),
     "in1": ("sbuf", [P, COLS], "bfloat16"),
     "ys": ("sbuf", [P, COLS], "bfloat16"),
-    "acc0": ("psum", [P, COLS], "float32"),
-    "acc1": ("psum", [P, COLS], "float32"),
 }
+for _i in range(NG):
+    SCRATCH["acc%d" % _i] = ("psum", [P, COLS], "float32")
 for _i, _w in enumerate(PARTS):
     SCRATCH["part%d" % _i] = ("dram", [P, _w], "bfloat16")
-SEMAPHORES = (["ld_s", "ld_x", "ld_w", "sent", "mm0", "mm1", "cp0", "cp1", "st0", "st1"]
+SEMAPHORES = (["ld_s", "ld_x", "ld_w", "sent"]
+              + ["%s%d" % (n, i) for n in ("mm", "cp", "st") for i in range(NG)]
               + ["a%d" % k for k in range(NSRC)] + ["l%d" % p for p in range(len(PARTS))]
+              + ["a%d_%d" % (k, i) for k in range(NSRC) for i in range(NG)]
               + ["f%d_%d" % (k, p) for k in range(NSRC) for p in range(len(PARTS))])
 
 _CACHE = {}
@@ -96,34 +103,55 @@ def _plan(T, topo):
         for d in cons:
             depth[(d, j)] = 1 if d in direct else 2
         entry = [c for c in world if rack(c) != rack(s) and topo.chip(c) == topo.chip(s) and topo.may_write(s, c)]
-        eng = common(s, entry[:1])
-        cable, local = eng[:len(eng) // 2], eng[len(eng) // 2:]
-        teams = []
-        if far:
-            teams.append((team(entry[0], dies, s, far), cable, far))
-        if cross:
-            teams.append((team(s, dies, s, cross), local, cross))
-        heads, bodies = [], []
+        off = common(s, entry[:1])
+        cable, switch = off[:len(off) // 2], off[len(off) // 2:]
+        away_team = team(entry[0], dies, s, far) if far else []
+        mate = [c for c in world if topo.mates(c, s)][:1]
+        home_team = team(s, dies, s, cross + mate)
+        inner = [b for b in common(s, home_team) if b not in off][:len(cable)]
+        share = len(cable) // NHEAD
+        heads, early, bodies = [], [], []
         for p in range(len(PARTS)):
             f = "f%d_%d" % (k, p)
-            if p >= NHEAD:
-                bodies.append([])
-            for relays, mine, targets in teams:
-                h = relays[p % len(relays)]
-                share = len(mine) // NHEAD
-                use = mine[p * share:(p + 1) * share] if p < NHEAD else mine
-                (heads if p < NHEAD else bodies[-1]).append((use, [h], p, f))
-                steps.setdefault(h, []).append(((f, len(use)), fan(h, targets, p, name)))
-        calls = [heads] + bodies + [[(local, [d], None, name)] for d in direct]
+            fr = away_team[p % len(away_team)] if far else None
+            hr = home_team[p % len(home_team)]
+            if p < NHEAD:
+                if far:
+                    heads.append((cable[p * share:(p + 1) * share], [fr], p, f))
+                    steps.setdefault(fr, []).append(((f, share), fan(fr, far, p, name)))
+                if cross:
+                    heads.append((inner[p * share:(p + 1) * share], [hr], p, f))
+                    steps.setdefault(hr, []).append(((f, share), fan(hr, cross, p, name)))
+            elif far and p in DELEG:
+                w = len(inner) // len(DELEG)
+                i = DELEG.index(p)
+                early.append((inner[i * w:(i + 1) * w], [hr], p, f))
+                out = common(hr, [fr])
+                out = out[:len(out) // 2]
+                steps.setdefault(hr, []).insert(0, ((f, w), [(out, [fr], p, f)]))
+                steps.setdefault(fr, []).append(((f, len(out)), fan(fr, far, p, name)))
+                if cross:
+                    steps[hr].append(((f, w), fan(hr, cross, p, name)))
+            else:
+                call = []
+                if far:
+                    call.append((cable, [fr], p, f))
+                    steps.setdefault(fr, []).append(((f, len(cable)), fan(fr, far, p, name)))
+                if cross:
+                    call.append((inner, [hr], p, f))
+                    steps.setdefault(hr, []).append(((f, len(inner)), fan(hr, cross, p, name)))
+                bodies.append(call)
+        calls = [c for c in [heads, early] + bodies if c] + [[(switch, [d], None, name)] for d in direct]
         steps.setdefault(s, []).extend((None, call) for call in calls)
 
     arrive = {}
     for c, todo in steps.items():
         for _, call in todo:
-            for eng, dests, _, name in call:
+            for eng, dests, part, name in call:
                 for d in dests:
                     if d in group:
-                        arrive[(d, name)] = arrive.get((d, name), 0) + len(eng)
+                        key = (d, name, None if part is None else GROUP_OF[part])
+                        arrive[key] = arrive.get(key, 0) + len(eng)
     return {"steps": steps, "arrive": arrive, "depth": depth, "sem": {j: "a%d" % k for k, j in enumerate(sources)},
             "src": {"a%d" % k: j for k, j in enumerate(sources)}}
 
@@ -175,8 +203,9 @@ def rank_program(g, core, T, topo):
         transfers = []
         for eng, dests, part, name in call:
             dsts = []
+            to_rank = T.rank_of(dests[0]) is not None
             for d in dests:
-                if T.rank_of(d) is None:
+                if not to_rank:
                     dsts.append(whole_or_part(part))
                 elif part is None:
                     dsts.append(landing(d, plan["src"][name])[:])
@@ -186,7 +215,8 @@ def rank_program(g, core, T, topo):
             transfers.append(RemoteDMATransfer(
                 dst_ids=[DstId(rid=rid, pnc=pid) for rid, pid in ids],
                 dma_engine_mask=sum(1 << b for b in eng),
-                remote_sem=sem[name], srcs=[whole_or_part(part)], dsts=dsts))
+                remote_sem=sem["%s_%d" % (name, GROUP_OF[part])] if to_rank and part is not None else sem[name],
+                srcs=[whole_or_part(part)], dsts=dsts))
             sent += len(eng)
         g.remote_dma_fused(transfers, local_sem=sem.sent)
     if sent:
@@ -195,25 +225,40 @@ def rank_program(g, core, T, topo):
     if rank is None:
         return
     order = sorted(range(len(table[rank])), key=lambda i: plan["depth"].get((core, table[rank][i]), 0))
+
+    def multiply(i, q):
+        j = table[rank][i]
+        rhs = T.xs if j == rank else landing(core, j)
+        mm = g.tensor.matmul(T["acc%d" % q][:, 0:GWIDTH[q]], T.ws[:, TILE * i:TILE * (i + 1)],
+                             rhs[:, GSTART[q]:GSTART[q] + GWIDTH[q]], start=(i == order[0]), stop=(i == order[-1]))
+        if i == order[-1]:
+            mm.then_inc(sem["mm%d" % q], 1)
+
     g.tensor.wait_ge(sem.ld_w, 16)
-    for pos, i in enumerate(order):
+    late = []
+    for i in order:
         j = table[rank][i]
         if j == rank:
             g.tensor.wait_ge(sem.ld_x, 16)
-            rhs = T.xs
+        elif (core, plan["sem"][j], None) in plan["arrive"]:
+            g.tensor.wait_ge(sem[plan["sem"][j]], plan["arrive"][(core, plan["sem"][j], None)])
         else:
-            g.tensor.wait_ge(sem[plan["sem"][j]], plan["arrive"][(core, plan["sem"][j])])
-            rhs = landing(core, j)
-        for h in range(2):
-            mm = g.tensor.matmul(T["acc%d" % h][:, 0:HALF], T.ws[:, TILE * i:TILE * (i + 1)],
-                                 rhs[:, HALF * h:HALF * (h + 1)], start=(pos == 0), stop=(pos == len(order) - 1))
-            if pos == len(order) - 1:
-                mm.then_inc(sem["mm%d" % h], 1)
-    for h in range(2):
-        g.vector.wait_ge(sem["mm%d" % h], 1)
-        g.vector.tensor_copy(T.ys[:, HALF * h:HALF * (h + 1)], T["acc%d" % h][:, 0:HALF]).then_inc(sem["cp%d" % h], 1)
-    for h in range(2):
-        queues[h].wait_ge(sem["cp%d" % h], 1)
-        queues[h].dma_start(T.y[:, HALF * h:HALF * (h + 1)],
-                            T.ys[:, HALF * h:HALF * (h + 1)]).then_inc(sem["st%d" % h], 16)
-        queues[h].wait_ge(sem["st%d" % h], 16)
+            late.append(i)
+            continue
+        for q in range(NG):
+            multiply(i, q)
+    for q in range(NG):
+        for i in late:
+            name = plan["sem"][table[rank][i]]
+            g.tensor.wait_ge(sem["%s_%d" % (name, q)], plan["arrive"][(core, name, q)])
+            multiply(i, q)
+    for q in range(NG):
+        g.vector.wait_ge(sem["mm%d" % q], 1)
+        g.vector.tensor_copy(T.ys[:, GSTART[q]:GSTART[q] + GWIDTH[q]],
+                             T["acc%d" % q][:, 0:GWIDTH[q]]).then_inc(sem["cp%d" % q], 1)
+    for q in range(NG):
+        queues[q % 2].wait_ge(sem["cp%d" % q], 1)
+        queues[q % 2].dma_start(T.y[:, GSTART[q]:GSTART[q] + GWIDTH[q]],
+                                T.ys[:, GSTART[q]:GSTART[q] + GWIDTH[q]]).then_inc(sem["st%d" % q], 16)
+    for q in range(NG):
+        queues[q % 2].wait_ge(sem["st%d" % q], 16)

from concourse.bass import DstId, RemoteDMATransfer

SIM_CORES = 512
P, COLS, TILE = 128, 512, 128
NREL = 4
NHEAD = 4
PARTS = [32, 32, 32, 32, 80, 64, 120, 120]
DELEG = (6, 7)
STARTS = [sum(PARTS[:i]) for i in range(len(PARTS))]
GROUPS = [list(range(NHEAD))] + [[p] for p in range(NHEAD, len(PARTS))]
GROUP_OF = {p: i for i, ps in enumerate(GROUPS) for p in ps}
GSTART = [STARTS[ps[0]] for ps in GROUPS]
GWIDTH = [sum(PARTS[p] for p in ps) for ps in GROUPS]
NG = len(GROUPS)
NSRC = 3

SCRATCH = {
    "stage": ("dram", [P, COLS], "bfloat16"),
    "xs": ("sbuf", [P, COLS], "bfloat16"),
    "ws": ("sbuf", [P, 3 * TILE], "bfloat16"),
    "in0": ("sbuf", [P, COLS], "bfloat16"),
    "in1": ("sbuf", [P, COLS], "bfloat16"),
    "ys": ("sbuf", [P, COLS], "bfloat16"),
}
for _i in range(NG):
    SCRATCH["acc%d" % _i] = ("psum", [P, COLS], "float32")
for _i, _w in enumerate(PARTS):
    SCRATCH["part%d" % _i] = ("dram", [P, _w], "bfloat16")
SEMAPHORES = (["ld_s", "ld_x", "ld_w", "sent"]
              + ["%s%d" % (n, i) for n in ("mm", "cp", "st") for i in range(NG)]
              + ["a%d" % k for k in range(NSRC)] + ["l%d" % p for p in range(len(PARTS))]
              + ["a%d_%d" % (k, i) for k in range(NSRC) for i in range(NG)]
              + ["f%d_%d" % (k, p) for k in range(NSRC) for p in range(len(PARTS))])

_CACHE = {}


def _bits(m):
    return [b for b in range(m.bit_length()) if (m >> b) & 1]


def _plan(T, topo):
    cores = list(T.cores)
    group = set(cores)
    table = T.tables["MASK"]
    n = len(cores)
    world = range(SIM_CORES)

    def place(c):
        return (topo.host(c), topo.chip(c))

    def rack(c):
        return topo.rack(topo.host(c))

    def common(c, dests):
        m = -1
        for d in dests:
            m &= topo.mask(c, d)
        return _bits(m)

    sources = [j for j in range(n) if any(j in table[r] for r in range(n) if r != j)]
    used = set()
    steps = {}
    depth = {}

    def team(at, dies, feeder, targets):
        out = []
        for i in range(NREL):
            cand = [c for c in world if place(c) == place(at) and c not in group and c not in used
                    and topo.may_write(feeder, c) and all(topo.may_write(c, t) for t in targets)]
            if cand:
                cand.sort(key=lambda c: (topo.die(c) != dies[i % len(dies)], c))
                used.add(cand[0])
                out.append(cand[0])
        return out

    def fan(h, targets, part, name):
        away = [t for t in targets if place(t) != place(h)]
        here = [t for t in targets if place(t) == place(h)]
        eng = common(h, away)
        half = len(eng) // 2
        if len(away) % 2:
            call = [(eng, away, part, name)]
        else:
            call = [(eng[:half], away[0::2], part, name), (eng[half:], away[1::2], part, name)]
        if here:
            spare = [b for b in common(h, here) if b not in eng]
            call.append((spare[:len(eng) // 4], here, part, name))
        return call

    for k, j in enumerate(sources):
        s = cores[j]
        name = "a%d" % k
        cons = sorted(cores[r] for r in range(n) if r != j and j in table[r])
        own = topo.die(s)
        other = [d for d in sorted({topo.die(c) for c in world if place(c) == place(s)}) if d != own][0]
        dies = (other, own) if k % 2 else (own, other)

        near = [d for d in cons if rack(d) == rack(s)]
        far = [d for d in cons if rack(d) != rack(s)]
        direct = [d for d in near if topo.may_write(s, d)]
        cross = [d for d in near if not topo.may_write(s, d)]
        for d in cons:
            depth[(d, j)] = 1 if d in direct else 2
        entry = [c for c in world if rack(c) != rack(s) and topo.chip(c) == topo.chip(s) and topo.may_write(s, c)]
        off = common(s, entry[:1])
        cable, switch = off[:len(off) // 2], off[len(off) // 2:]
        away_team = team(entry[0], dies, s, far) if far else []
        mate = [c for c in world if topo.mates(c, s)][:1]
        home_team = team(s, dies, s, cross + mate)
        inner = [b for b in common(s, home_team) if b not in off][:len(cable)]
        share = len(cable) // NHEAD
        heads, early, bodies = [], [], []
        for p in range(len(PARTS)):
            f = "f%d_%d" % (k, p)
            fr = away_team[p % len(away_team)] if far else None
            hr = home_team[p % len(home_team)]
            if p < NHEAD:
                if far:
                    heads.append((cable[p * share:(p + 1) * share], [fr], p, f))
                    steps.setdefault(fr, []).append(((f, share), fan(fr, far, p, name)))
                if cross:
                    heads.append((inner[p * share:(p + 1) * share], [hr], p, f))
                    steps.setdefault(hr, []).append(((f, share), fan(hr, cross, p, name)))
            elif far and p in DELEG:
                w = len(inner) // len(DELEG)
                i = DELEG.index(p)
                early.append((inner[i * w:(i + 1) * w], [hr], p, f))
                out = common(hr, [fr])
                out = out[:len(out) // 2]
                steps.setdefault(hr, []).insert(0, ((f, w), [(out, [fr], p, f)]))
                steps.setdefault(fr, []).append(((f, len(out)), fan(fr, far, p, name)))
                if cross:
                    steps[hr].append(((f, w), fan(hr, cross, p, name)))
            else:
                call = []
                if far:
                    call.append((cable, [fr], p, f))
                    steps.setdefault(fr, []).append(((f, len(cable)), fan(fr, far, p, name)))
                if cross:
                    call.append((inner, [hr], p, f))
                    steps.setdefault(hr, []).append(((f, len(inner)), fan(hr, cross, p, name)))
                bodies.append(call)
        calls = [c for c in [heads, early] + bodies if c] + [[(switch, [d], None, name)] for d in direct]
        steps.setdefault(s, []).extend((None, call) for call in calls)

    arrive = {}
    for c, todo in steps.items():
        for _, call in todo:
            for eng, dests, part, name in call:
                for d in dests:
                    if d in group:
                        key = (d, name, None if part is None else GROUP_OF[part])
                        arrive[key] = arrive.get(key, 0) + len(eng)
    return {"steps": steps, "arrive": arrive, "depth": depth, "sem": {j: "a%d" % k for k, j in enumerate(sources)},
            "src": {"a%d" % k: j for k, j in enumerate(sources)}}


def rank_program(g, core, T, topo):
    if "plan" not in _CACHE:
        _CACHE["plan"] = _plan(T, topo)
    plan = _CACHE["plan"]
    table = T.tables["MASK"]
    rank = T.rank_of(core)
    todo = plan["steps"].get(core, [])
    if rank is None and not todo:
        return
    sem = T.sem

    def landing(c, j):
        r = T.rank_of(c)
        return T["in%d" % [m for m in table[r] if m != r].index(j)]

    def whole_or_part(part):
        return T.stage[:] if part is None else T["part%d" % part][:]

    def staged(part):
        return sem.ld_s if part is None else sem["l%d" % part]

    queues = [g.sync, g.scalar]
    if rank is not None:
        pieces = []
        for _, call in todo:
            for t in call:
                if t[2] not in pieces:
                    pieces.append(t[2])
        for q, p in enumerate(pieces):
            cols = T.x[:] if p is None else T.x[:, STARTS[p]:STARTS[p] + PARTS[p]]
            queues[q % 2].dma_start(whole_or_part(p), cols).then_inc(staged(p), 16)
        queues[len(pieces) % 2].dma_start(T.xs[:], T.x[:]).then_inc(sem.ld_x, 16)
        queues[(len(pieces) + 1) % 2].dma_start(T.ws[:], T.w[:]).then_inc(sem.ld_w, 16)

    sent = 0
    waited = []
    for wait, call in todo:
        if wait is None:
            for t in call:
                if t[2] not in waited:
                    waited.append(t[2])
                    g.wait_ge(staged(t[2]), 16)
        else:
            g.wait_ge(sem[wait[0]], wait[1])
        transfers = []
        for eng, dests, part, name in call:
            dsts = []
            to_rank = T.rank_of(dests[0]) is not None
            for d in dests:
                if not to_rank:
                    dsts.append(whole_or_part(part))
                elif part is None:
                    dsts.append(landing(d, plan["src"][name])[:])
                else:
                    dsts.append(landing(d, plan["src"][name])[:, STARTS[part]:STARTS[part] + PARTS[part]])
            ids = [topo.addr(d, core) for d in dests]
            transfers.append(RemoteDMATransfer(
                dst_ids=[DstId(rid=rid, pnc=pid) for rid, pid in ids],
                dma_engine_mask=sum(1 << b for b in eng),
                remote_sem=sem["%s_%d" % (name, GROUP_OF[part])] if to_rank and part is not None else sem[name],
                srcs=[whole_or_part(part)], dsts=dsts))
            sent += len(eng)
        g.remote_dma_fused(transfers, local_sem=sem.sent)
    if sent:
        g.wait_ge(sem.sent, sent)

    if rank is None:
        return
    order = sorted(range(len(table[rank])), key=lambda i: plan["depth"].get((core, table[rank][i]), 0))

    def multiply(i, q):
        j = table[rank][i]
        rhs = T.xs if j == rank else landing(core, j)
        mm = g.tensor.matmul(T["acc%d" % q][:, 0:GWIDTH[q]], T.ws[:, TILE * i:TILE * (i + 1)],
                             rhs[:, GSTART[q]:GSTART[q] + GWIDTH[q]], start=(i == order[0]), stop=(i == order[-1]))
        if i == order[-1]:
            mm.then_inc(sem["mm%d" % q], 1)

    g.tensor.wait_ge(sem.ld_w, 16)
    late = []
    for i in order:
        j = table[rank][i]
        if j == rank:
            g.tensor.wait_ge(sem.ld_x, 16)
        elif (core, plan["sem"][j], None) in plan["arrive"]:
            g.tensor.wait_ge(sem[plan["sem"][j]], plan["arrive"][(core, plan["sem"][j], None)])
        else:
            late.append(i)
            continue
        for q in range(NG):
            multiply(i, q)
    for q in range(NG):
        for i in late:
            name = plan["sem"][table[rank][i]]
            g.tensor.wait_ge(sem["%s_%d" % (name, q)], plan["arrive"][(core, name, q)])
            multiply(i, q)
    for q in range(NG):
        g.vector.wait_ge(sem["mm%d" % q], 1)
        g.vector.tensor_copy(T.ys[:, GSTART[q]:GSTART[q] + GWIDTH[q]],
                             T["acc%d" % q][:, 0:GWIDTH[q]]).then_inc(sem["cp%d" % q], 1)
    for q in range(NG):
        queues[q % 2].wait_ge(sem["cp%d" % q], 1)
        queues[q % 2].dma_start(T.y[:, GSTART[q]:GSTART[q] + GWIDTH[q]],
                                T.ys[:, GSTART[q]:GSTART[q] + GWIDTH[q]]).then_inc(sem["st%d" % q], 16)
    for q in range(NG):
        queues[q % 2].wait_ge(sem["st%d" % q], 16)
